import numpy as np
import ml_dtypes


def mxq(x, axis, fmt="e4m3"):
    dtype, down = {"e4m3": (ml_dtypes.float8_e4m3fn, 7), "e5m2": (ml_dtypes.float8_e5m2, 14)}[fmt]
    v = np.moveaxis(np.asarray(x, np.float32).astype(ml_dtypes.bfloat16).astype(np.float64), axis, -1)
    blocks = v.reshape(v.shape[:-1] + (-1, 32))
    amax = np.abs(blocks).max(-1, keepdims=True)
    byte = np.maximum(np.where(amax > 0, np.frexp(amax)[1] - 1 + 127, 0) - down, 1)
    scale = np.exp2(byte - 127.0)
    codes = (blocks / scale).astype(np.float32).astype(dtype).astype(np.float64)
    return np.moveaxis((codes * scale).reshape(v.shape), -1, axis)


WIDE = False


def mx_kscale(k):
    if not WIDE:
        return np.ones(k)
    levels = np.array([30, -30])
    if k % 512:
        return np.exp2(np.random.permutation(np.resize(levels, k // 32))).repeat(32)
    a = np.empty((k // 512, 16))
    for p in range(k // 512):
        a[p, :8] = np.random.permutation(np.resize(levels, 8))
        for g in range(8):
            far = levels[np.abs(levels - a[p, g]) >= 10]
            a[p, g + 8] = far[np.random.randint(len(far))]
    return np.exp2(a.ravel()).repeat(32)


def f64(x):
    return np.asarray(x).astype(np.float64)


def striped(idx):
    return np.tile(np.asarray(idx).reshape(-1, 16).T, (8, 1)).astype(np.uint16)


def unstriped(offs):
    return offs[:16].T.reshape(-1).astype(np.int64)


E2M1 = np.array([0.0, 0.5, 1.0, 1.5, 2.0, 3.0, 4.0, 6.0, -0.0, -0.5, -1.0, -1.5, -2.0, -3.0, -4.0, -6.0])


def pack_weight(w, fmt):
    k, n = w.shape
    w = f64(np.asarray(w, np.float32).astype(ml_dtypes.bfloat16)).reshape(k // 32, 32, n)
    amax = np.abs(w).max(1)
    if fmt in ("e4m3", "e5m2"):
        byte = np.frexp(amax)[1] - 1 + 127 - (7 if fmt == "e4m3" else 14)
    else:
        mant, ex = np.frexp(amax / 6.0)
        byte = np.where(mant > 0.5, ex, ex - 1) + 127
    byte = np.clip(np.where(amax > 0, byte, 1), 1, 254)
    scaled = (w * np.exp2(127.0 - byte)[:, None, :]).reshape(k, n).astype(np.float32)
    by_word = np.ascontiguousarray(scaled.reshape(k // 512, 128, 4, n).transpose(0, 1, 3, 2))
    if fmt in ("e4m3", "e5m2"):
        words = by_word.astype(ml_dtypes.float8_e4m3fn if fmt == "e4m3" else ml_dtypes.float8_e5m2).view(np.uint8)
    else:
        c = by_word.astype(ml_dtypes.float4_e2m1fn).view(np.uint8) & 0xF
        words = (c[..., 0::2] | (c[..., 1::2] << 4)).reshape(k // 512, 128, 2 * n)
    return np.ascontiguousarray(words), np.ascontiguousarray(byte.astype(np.uint8).reshape(k // 512, 16, n))


def unpack_weight(words, scales, fmt):
    g, _, n = scales.shape
    words = np.ascontiguousarray(words).reshape(g, 128, n, -1)
    if fmt in ("e4m3", "e5m2"):
        vals = words.view(ml_dtypes.float8_e4m3fn if fmt == "e4m3" else ml_dtypes.float8_e5m2).astype(np.float64)
    else:
        nib = np.empty((g, 128, n, 4), np.uint8)
        nib[..., 0::2] = words & 0xF
        nib[..., 1::2] = words >> 4
        vals = E2M1[nib]
    vals = vals * np.repeat(np.exp2(scales.astype(np.float64) - 127.0), 8, axis=1)[..., None]
    return vals.transpose(0, 1, 3, 2).reshape(g * 512, n)


def sigmoid(v):
    return 1.0 / (1.0 + np.exp(-v))


def sgn(shape):
    return np.random.uniform(0.5, 2.0, shape) * np.where(np.random.standard_normal(shape) < 0, -1.0, 1.0)


K, T, J, R, F, Z, N, C, O = 512, 1024, 256, 512, 512, 1024, 256, 512, 128


def setup_inputs():
    n = np.random.standard_normal
    idx = np.random.permutation(T)[:J]
    idx2 = np.random.permutation(Z)[:J]
    idx3 = np.random.permutation(C)[:J]
    idx4 = np.random.permutation(C)[:J]
    idx5 = np.random.permutation(J)[:O]
    idx6 = np.random.permutation(J)[:O]
    ff = mx_kscale(F)
    fk = mx_kscale(K)
    fr = mx_kscale(R)
    xop = pack_weight(n((F, Z)) / ff[:, None], "e5m2")
    wp = pack_weight(n((K, R)) * 1 / np.sqrt(K) / fk[:, None] * fr, "e5m2")
    w2p = pack_weight(n((F, R)) * 1 / np.sqrt(F) * ff[:, None] * fr, "e4m3")
    wbp = pack_weight(n((R, N)) * 1 / np.sqrt(R) / fr[:, None], "e4m3")
    wcp = pack_weight(n((R, N)) * 1 / np.sqrt(R) / fr[:, None], "e2m1")
    return {
        "xo_words": xop[0],
        "xo_scales": xop[1],
        "cq": (np.random.randint(-7, 8, (K, T)).astype(np.float64)).astype(np.float32),
        "gs": (np.random.uniform(0.1, 0.4, (K, 1)) * fk[:, None]).astype(np.float32),
        "w_words": wp[0],
        "w_scales": wp[1],
        "w2_words": w2p[0],
        "w2_scales": w2p[1],
        "wb_words": wbp[0],
        "wb_scales": wbp[1],
        "wc_words": wcp[0],
        "wc_scales": wcp[1],
        "so": (np.random.uniform(0.5, 1.6, (N, 1))).astype(np.float32),
        "sp": (sgn((N, 1))).astype(np.float32),
        "bo": (np.random.uniform(-2.0, 2.0, (N, 1))).astype(np.float32),
        "offs": striped(idx),
        "offs2": striped(idx2),
        "offs3": striped(idx3),
        "offs4": striped(idx4),
        "offs5": striped(idx5),
        "offs6": striped(idx6),
    }


def reference(xo_words, xo_scales, cq, gs, w_words, w_scales, w2_words, w2_scales, wb_words, wb_scales, wc_words, wc_scales, so, sp, bo, offs, offs2, offs3, offs4, offs5, offs6):
    idx = unstriped(offs)
    idx2 = unstriped(offs2)
    idx3 = unstriped(offs3)
    idx4 = unstriped(offs4)
    idx5 = unstriped(offs5)
    idx6 = unstriped(offs6)
    xou = unpack_weight(xo_words, xo_scales, "e5m2")
    wu = unpack_weight(w_words, w_scales, "e5m2")
    w2u = unpack_weight(w2_words, w2_scales, "e4m3")
    wbu = unpack_weight(wb_words, wb_scales, "e4m3")
    wcu = unpack_weight(wc_words, wc_scales, "e2m1")
    x1 = f64(cq)[:, idx] * f64(gs)
    x1q = mxq(x1, 0, "e4m3")
    a = wu.T @ x1q
    xoidx2g = xou[:, idx2]
    b = w2u.T @ xoidx2g
    hid = np.maximum(a, b)
    hidq = mxq(hid, 0, "e5m2")
    p = wbu.T @ hidq
    q = wcu.T @ hidq
    pw = np.zeros((N, C))
    pw[:, idx3] = p
    m0 = np.maximum(pw[:, idx4], q)
    y = m0[:, idx5] * f64(so) * sigmoid(m0[:, idx6] * f64(sp) + f64(bo))
    return y

@@ -1,0 +1,240 @@
+from contextlib import ExitStack
+
+import concourse.mybir as mybir
+
+K, T, J, R, F, Z, N, C, O = 512, 1024, 256, 512, 512, 1024, 256, 512, 128
+FLOPS = 2 * J * (K * R + F * R + 2 * R * N)
+
+F32 = mybir.dt.float32
+BF16 = mybir.dt.bfloat16
+I32 = mybir.dt.int32
+U32 = mybir.dt.uint32
+U16 = mybir.dt.uint16
+U8 = mybir.dt.uint8
+E4M3 = mybir.dt.float8_e4m3fn_x4
+E5M2 = mybir.dt.float8_e5m2_x4
+E2M1 = mybir.dt.float4_e2m1fn_x4
+ACT = mybir.ActivationFunctionType
+ALU = mybir.AluOpType
+
+P = 128
+PACK = 4
+QUADS = 4
+HALVES = 2
+JH = J // HALVES
+NT = N // P
+LIST_ROWS = 16
+
+
+def tile_list_outcomegatedchain_codednote_kernel(
+    tc, xo_words, xo_scales, cq, gs, w_words, w_scales, w2_words, w2_scales, wb_words, wb_scales,
+    wc_words, wc_scales, so, sp, bo, offs, offs2, offs3, offs4, offs5, offs6, out,
+):
+    nc = tc.nc
+    with ExitStack() as ctx:
+        sb = ctx.enter_context(tc.tile_pool(name="sb", bufs=1))
+        ps = ctx.enter_context(tc.psum_pool(name="ps", bufs=1))
+
+        def tile(shape, dtype, name, tag=None):
+            return sb.tile(shape, dtype, name=name, tag=tag or name, align_bytes=64)
+
+        def load_list(src, name):
+            t = sb.tile(list(src.shape), U16, name=name)
+            nc.sync.dma_start(out=t[:], in_=src)
+            return t
+
+        def load_words(src, name):
+            flat = src[0] if src.ndim == 3 else src[0].rearrange("p c t -> p (c t)")
+            t = tile([P, flat.shape[1] // 4], I32, name)
+            nc.sync.dma_start(out=t[:], in_=flat.bitcast(I32))
+            return t
+
+        def load_scale_rows(queue, src, name):
+            width = src.shape[2] // 4
+            t = tile([PACK, QUADS, width], I32, name)
+            queue.dma_start(out=t[:], in_=src[0].bitcast(I32).rearrange("(q r) w -> r q w", r=PACK))
+            return t
+
+        def zeroed_plane(width, name, tag=None):
+            t = tile([P, width], U8, name, tag)
+            nc.vector.memset(t[:].bitcast(I32), 0)
+            return t
+
+        def spread(plane, rows):
+            for q in range(QUADS):
+                nc.vector.tensor_copy(out=plane[32 * q : 32 * q + PACK, :].bitcast(I32), in_=rows[:, q, :])
+
+        def dealt(dst):
+            return dst.rearrange("p (t m) -> p m t", t=PACK)
+
+        def undealt(src):
+            return src.rearrange("p (m t) -> p m t", t=PACK)
+
+        def half(lst, h):
+            cols = JH // LIST_ROWS
+            return lst[:, h * cols : (h + 1) * cols]
+
+        l2 = load_list(offs2, "l2")
+        l1 = load_list(offs, "l1")
+        xo_rows = load_scale_rows(nc.scalar, xo_scales, "xo_rows")
+        w2_rows = load_scale_rows(nc.scalar, w2_scales, "w2_rows")
+        xo_w = load_words(xo_words, "xo_w")
+        w2_w = load_words(w2_words, "w2_w")
+        cq_rows = cq.rearrange("(p t) c -> p t c", t=PACK)
+        cq_t = []
+        for t in range(PACK):
+            ct = tile([P, T], F32, "cq%d" % t)
+            nc.sync.dma_start(out=ct[:], in_=cq_rows[:, t, :])
+            cq_t.append(ct)
+        w_w = load_words(w_words, "w_w")
+        l3 = load_list(offs3, "l3")
+        wb_w = load_words(wb_words, "wb_w")
+        wc_w = load_words(wc_words, "wc_w")
+        l4 = load_list(offs4, "l4")
+        l5 = load_list(offs5, "l5")
+        l6 = load_list(offs6, "l6")
+
+        gs_t = tile([P, PACK], F32, "gs_t")
+        nc.gpsimd.dma_start(out=gs_t[:], in_=gs.rearrange("(p t) o -> p (t o)", t=PACK))
+        w_rows = load_scale_rows(nc.gpsimd, w_scales, "w_rows")
+        out_rows = tile([PACK, QUADS, 2 * N // 4], I32, "out_rows")
+        for u, src in enumerate((wb_scales, wc_scales)):
+            nc.gpsimd.dma_start(
+                out=out_rows[:, :, u * N // 4 : (u + 1) * N // 4],
+                in_=src[0].bitcast(I32).rearrange("(q r) w -> r q w", r=PACK),
+            )
+        per_n = []
+        with nc.allow_non_contiguous_dma(reason="one float32 value for each output feature"):
+            for src, name in ((sp, "sp_t"), (bo, "bo_t"), (so, "so_t")):
+                vt = tile([P, NT], F32, name)
+                nc.gpsimd.dma_start(out=vt[:], in_=src.rearrange("(i p) o -> p (i o)", p=P))
+                per_n.append(vt)
+        sp_t, bo_t, so_t = per_n
+
+        xo_plane = zeroed_plane(Z, "xo_plane")
+        w2_plane = zeroed_plane(R, "w2_plane")
+        boards = []
+        for i in range(NT):
+            bd = tile([P, C], F32, "board%d" % i)
+            nc.vector.memset(bd[:], 0.0)
+            boards.append(bd)
+
+        spread(xo_plane, xo_rows)
+        spread(w2_plane, w2_rows)
+        xg_s = tile([P, J], U8, "xg_s")
+        nc.vector.tensor_copy(out=xg_s[:], in_=xo_plane[:].indirect(l2[:]))
+        w2_s = tile([P, R], U8, "w2_s")
+        nc.vector.tensor_copy(out=dealt(w2_s[:]), in_=undealt(w2_plane[:]))
+        xg_w = tile([P, J], U32, "xg_w")
+        nc.vector.tensor_copy(out=xg_w[:], in_=xo_w[:].bitcast(U32).indirect(l2[:]))
+        w2_d = tile([P, R], I32, "w2_d")
+        nc.vector.tensor_copy(out=dealt(w2_d[:]), in_=undealt(w2_w[:]))
+        w_plane = zeroed_plane(R, "w_plane", "xo_w")
+        spread(w_plane, w_rows)
+        w_s = tile([P, R], U8, "w_s")
+        nc.vector.tensor_copy(out=dealt(w_s[:]), in_=undealt(w_plane[:]))
+        out_plane = zeroed_plane(2 * N, "out_plane", "w2_w")
+        spread(out_plane, out_rows)
+        wb_plane = out_plane[:, :N]
+        wc_plane = out_plane[:, N:]
+
+        b_sb = []
+        for h in range(HALVES):
+            js = slice(h * JH, (h + 1) * JH)
+            bank = ps.tile([P, PACK, JH], F32, name="b_ps%d" % h, tag="b_ps%d" % h)
+            for t in range(PACK):
+                ms = slice(t * P, (t + 1) * P)
+                nc.tensor.matmul_mx(
+                    out=bank[:, t, :], lhsT=w2_d[:, ms].bitcast(E4M3), lhsT_scale=w2_s[:, ms],
+                    rhs=xg_w[:, js].bitcast(E5M2), rhs_scale=xg_s[:, js], start=True, stop=True,
+                )
+            bs = tile([P, JH, PACK], F32, "b_sb%d" % h)
+            nc.vector.tensor_copy(out=bs[:], in_=bank[:].rearrange("p t j -> p j t"))
+            b_sb.append(bs)
+
+        x1 = tile([P, PACK, J], BF16, "x1")
+        for t in range(PACK):
+            nc.scalar.activation(
+                out=x1[:, t, :], in_=cq_t[t][:].indirect(l1[:]), func=ACT.Copy, scale=gs_t[:, t : t + 1]
+            )
+        w_d = tile([P, R], U32, "w_d")
+        nc.scalar.copy(out=dealt(w_d[:]), in_=undealt(w_w[:].bitcast(U32)))
+
+        a_ps = []
+        for h in range(HALVES):
+            js = slice(h * JH, (h + 1) * JH)
+            woven = tile([P, JH, PACK], BF16, "x1_woven%d" % h)
+            nc.vector.tensor_copy(out=woven[:], in_=x1[:, :, js].rearrange("p t j -> p j t"))
+            codes = tile([P, JH], U32, "x1_codes%d" % h)
+            scales = tile([P, JH], U8, "x1_scales%d" % h)
+            nc.vector.quantize_mx(
+                out=codes[:].bitcast(E4M3), scales=scales[:], in_=woven[:].rearrange("p j t -> p (j t)")
+            )
+            bank = ps.tile([P, PACK, JH], F32, name="a_ps%d" % h)
+            for t in range(PACK):
+                ms = slice(t * P, (t + 1) * P)
+                nc.tensor.matmul_mx(
+                    out=bank[:, t, :], lhsT=w_d[:, ms].bitcast(E5M2), lhsT_scale=w_s[:, ms],
+                    rhs=codes[:].bitcast(E4M3), rhs_scale=scales[:], start=True, stop=True,
+                )
+            a_ps.append(bank)
+
+        q_ps = ps.tile([P, NT, J], F32, name="q_ps")
+        wc_bytes = wc_w[:].bitcast(U8)
+        p_sb = []
+        for h in range(HALVES):
+            js = slice(h * JH, (h + 1) * JH)
+            hid = tile([P, JH, PACK], BF16, "hid%d" % h)
+            nc.vector.tensor_tensor(
+                out=hid[:], in0=a_ps[h][:].rearrange("p t j -> p j t"), in1=b_sb[h][:], op=ALU.max
+            )
+            codes = tile([P, JH], U32, "hid_codes%d" % h)
+            scales = tile([P, JH], U8, "hid_scales%d" % h)
+            nc.vector.quantize_mx(
+                out=codes[:].bitcast(E5M2), scales=scales[:], in_=hid[:].rearrange("p j t -> p (j t)")
+            )
+            p_ps = [
+                ps.tile([P, JH], F32, name="p_ps%d%d" % (h, i), tag=("b_ps%d" % i if h == 0 else "p_ps%d" % i))
+                for i in range(NT)
+            ]
+            for i in range(NT):
+                ns = slice(i * P, (i + 1) * P)
+                nc.tensor.matmul_mx(
+                    out=p_ps[i][:], lhsT=wb_w[:, ns].bitcast(E4M3), lhsT_scale=wb_plane[:, ns],
+                    rhs=codes[:].bitcast(E5M2), rhs_scale=scales[:], start=True, stop=True,
+                )
+            for i in range(NT):
+                ns = slice(i * P, (i + 1) * P)
+                nc.tensor.matmul_mx(
+                    out=q_ps[:, i, js], lhsT=wc_bytes[:, 2 * i * P : 2 * (i + 1) * P].bitcast(E2M1),
+                    lhsT_scale=wc_plane[:, ns],
+                    rhs=codes[:].bitcast(E5M2), rhs_scale=scales[:], start=True, stop=True,
+                )
+            pt = tile([P, JH], F32, "p_sb%d0" % h)
+            nc.scalar.copy(out=pt[:], in_=p_ps[0][:])
+            nc.scalar.activation(out=boards[0][:].indirect(half(l3, h)), in_=pt[:], func=ACT.Copy)
+            p_sb.append(p_ps[1])
+        for h in range(HALVES):
+            pt = tile([P, JH], F32, "p_sb%d1" % h)
+            nc.vector.tensor_copy(out=pt[:], in_=p_sb[h][:])
+            nc.vector.tensor_copy(out=boards[1][:].indirect(half(l3, h)), in_=pt[:])
+
+        picked = [tile([P, J], F32, "picked%d" % i) for i in range(NT)]
+        nc.scalar.activation(out=picked[0][:], in_=boards[0][:].indirect(l4[:]), func=ACT.Copy)
+        nc.vector.tensor_copy(out=picked[1][:], in_=boards[1][:].indirect(l4[:]))
+
+        for i in range(NT):
+            m0 = tile([P, J], F32, "m0_%d" % i)
+            nc.vector.tensor_tensor(out=m0[:], in0=q_ps[:, i, :], in1=picked[i][:], op=ALU.max)
+            gate = tile([P, O], F32, "gate%d" % i)
+            nc.scalar.activation(
+                out=gate[:], in_=m0[:].indirect(l6[:]), func=ACT.Sigmoid,
+                scale=sp_t[:, i : i + 1], bias=bo_t[:, i : i + 1],
+            )
+            kept = tile([P, O], F32, "kept%d" % i)
+            nc.scalar.activation(
+                out=kept[:], in_=m0[:].indirect(l5[:]), func=ACT.Copy, scale=so_t[:, i : i + 1]
+            )
+            y = tile([P, O], F32, "y%d" % i)
+            nc.vector.tensor_tensor(out=y[:], in0=kept[:], in1=gate[:], op=ALU.mult)
+            nc.sync.dma_start(out=out[i * P : (i + 1) * P, :], in_=y[:])

@@ -55,6 +55,16 @@ def tile_list_outcomegatedchain_codednote_kernel(
             queue.dma_start(out=t[:], in_=src[0].bitcast(I32).rearrange("(q r) w -> r q w", r=PACK))
             return t
 
+        def load_scale_pair(queue, first, second, name):
+            width = first.shape[2] // 4
+            t = tile([PACK, QUADS, 2 * width], I32, name)
+            for u, src in enumerate((first, second)):
+                queue.dma_start(
+                    out=t[:, :, u * width : (u + 1) * width],
+                    in_=src[0].bitcast(I32).rearrange("(q r) w -> r q w", r=PACK),
+                )
+            return t
+
         def zeroed_plane(width, name, tag=None):
             t = tile([P, width], U8, name, tag)
             nc.vector.memset(t[:].bitcast(I32), 0)
@@ -74,45 +84,46 @@ def tile_list_outcomegatedchain_codednote_kernel(
             cols = JH // LIST_ROWS
             return lst[:, h * cols : (h + 1) * cols]
 
-        l2 = load_list(offs2, "l2")
-        l1 = load_list(offs, "l1")
-        xo_rows = load_scale_rows(nc.scalar, xo_scales, "xo_rows")
-        w2_rows = load_scale_rows(nc.scalar, w2_scales, "w2_rows")
-        xo_w = load_words(xo_words, "xo_w")
-        w2_w = load_words(w2_words, "w2_w")
         cq_rows = cq.rearrange("(p t) c -> p t c", t=PACK)
-        cq_t = []
-        for t in range(PACK):
+
+        def load_cq(t):
             ct = tile([P, T], F32, "cq%d" % t)
             nc.sync.dma_start(out=ct[:], in_=cq_rows[:, t, :])
-            cq_t.append(ct)
-        w_w = load_words(w_words, "w_w")
-        l3 = load_list(offs3, "l3")
-        wb_w = load_words(wb_words, "wb_w")
-        wc_w = load_words(wc_words, "wc_w")
-        l4 = load_list(offs4, "l4")
-        l5 = load_list(offs5, "l5")
-        l6 = load_list(offs6, "l6")
+            return ct
 
         gs_t = tile([P, PACK], F32, "gs_t")
-        nc.gpsimd.dma_start(out=gs_t[:], in_=gs.rearrange("(p t) o -> p (t o)", t=PACK))
-        w_rows = load_scale_rows(nc.gpsimd, w_scales, "w_rows")
-        out_rows = tile([PACK, QUADS, 2 * N // 4], I32, "out_rows")
-        for u, src in enumerate((wb_scales, wc_scales)):
-            nc.gpsimd.dma_start(
-                out=out_rows[:, :, u * N // 4 : (u + 1) * N // 4],
-                in_=src[0].bitcast(I32).rearrange("(q r) w -> r q w", r=PACK),
-            )
+        nc.scalar.dma_start(out=gs_t[:], in_=gs.rearrange("(p t) o -> p (t o)", t=PACK))
+        xo_rows = load_scale_rows(nc.scalar, xo_scales, "xo_rows")
+        in_rows = load_scale_pair(nc.scalar, w_scales, w2_scales, "in_rows")
+        out_rows = load_scale_pair(nc.scalar, wb_scales, wc_scales, "out_rows")
+
+        l1 = load_list(offs, "l1")
+        cq_t = [load_cq(0), load_cq(1)]
+        l2 = load_list(offs2, "l2")
+        cq_t.extend([load_cq(2), load_cq(3)])
+        w_w = load_words(w_words, "w_w")
+        w2_w = load_words(w2_words, "w2_w")
+        xo_w = load_words(xo_words, "xo_w")
+        wb_w = load_words(wb_words, "wb_w")
+        wc_w = load_words(wc_words, "wc_w")
+        l3 = load_list(offs3, "l3")
+        l4 = load_list(offs4, "l4")
+        l6 = load_list(offs6, "l6")
+        l5 = load_list(offs5, "l5")
         per_n = []
         with nc.allow_non_contiguous_dma(reason="one float32 value for each output feature"):
             for src, name in ((sp, "sp_t"), (bo, "bo_t"), (so, "so_t")):
                 vt = tile([P, NT], F32, name)
-                nc.gpsimd.dma_start(out=vt[:], in_=src.rearrange("(i p) o -> p (i o)", p=P))
+                nc.sync.dma_start(out=vt[:], in_=src.rearrange("(i p) o -> p (i o)", p=P))
                 per_n.append(vt)
         sp_t, bo_t, so_t = per_n
 
         xo_plane = zeroed_plane(Z, "xo_plane")
-        w2_plane = zeroed_plane(R, "w2_plane")
+        in_plane = zeroed_plane(2 * R, "in_plane")
+        out_plane = zeroed_plane(2 * N, "out_plane")
+        idle = tile([P, 2], F32, "idle")
+        nc.vector.memset(idle[:, 0:1], 0.0)
+        nc.scalar.activation(out=idle[:, 1:2], in_=idle[:, 0:1], func=ACT.Sigmoid)
         boards = []
         for i in range(NT):
             bd = tile([P, C], F32, "board%d" % i)
@@ -120,37 +131,19 @@ def tile_list_outcomegatedchain_codednote_kernel(
             boards.append(bd)
 
         spread(xo_plane, xo_rows)
-        spread(w2_plane, w2_rows)
         xg_s = tile([P, J], U8, "xg_s")
         nc.vector.tensor_copy(out=xg_s[:], in_=xo_plane[:].indirect(l2[:]))
-        w2_s = tile([P, R], U8, "w2_s")
-        nc.vector.tensor_copy(out=dealt(w2_s[:]), in_=undealt(w2_plane[:]))
-        xg_w = tile([P, J], U32, "xg_w")
-        nc.vector.tensor_copy(out=xg_w[:], in_=xo_w[:].bitcast(U32).indirect(l2[:]))
-        w2_d = tile([P, R], I32, "w2_d")
-        nc.vector.tensor_copy(out=dealt(w2_d[:]), in_=undealt(w2_w[:]))
-        w_plane = zeroed_plane(R, "w_plane", "xo_w")
-        spread(w_plane, w_rows)
-        w_s = tile([P, R], U8, "w_s")
-        nc.vector.tensor_copy(out=dealt(w_s[:]), in_=undealt(w_plane[:]))
-        out_plane = zeroed_plane(2 * N, "out_plane", "w2_w")
+        spread(in_plane, in_rows)
+        in_s = tile([P, 2 * R], U8, "in_s")
+        nc.vector.tensor_copy(
+            out=in_s[:].rearrange("p (u t m) -> p u m t", u=2, t=PACK),
+            in_=in_plane[:].rearrange("p (u m t) -> p u m t", u=2, t=PACK),
+        )
+        w_s = in_s[:, :R]
+        w2_s = in_s[:, R:]
         spread(out_plane, out_rows)
         wb_plane = out_plane[:, :N]
         wc_plane = out_plane[:, N:]
-
-        b_sb = []
-        for h in range(HALVES):
-            js = slice(h * JH, (h + 1) * JH)
-            bank = ps.tile([P, PACK, JH], F32, name="b_ps%d" % h, tag="b_ps%d" % h)
-            for t in range(PACK):
-                ms = slice(t * P, (t + 1) * P)
-                nc.tensor.matmul_mx(
-                    out=bank[:, t, :], lhsT=w2_d[:, ms].bitcast(E4M3), lhsT_scale=w2_s[:, ms],
-                    rhs=xg_w[:, js].bitcast(E5M2), rhs_scale=xg_s[:, js], start=True, stop=True,
-                )
-            bs = tile([P, JH, PACK], F32, "b_sb%d" % h)
-            nc.vector.tensor_copy(out=bs[:], in_=bank[:].rearrange("p t j -> p j t"))
-            b_sb.append(bs)
 
         x1 = tile([P, PACK, J], BF16, "x1")
         for t in range(PACK):
@@ -160,7 +153,7 @@ def tile_list_outcomegatedchain_codednote_kernel(
         w_d = tile([P, R], U32, "w_d")
         nc.scalar.copy(out=dealt(w_d[:]), in_=undealt(w_w[:].bitcast(U32)))
 
-        a_ps = []
+        a_sb = []
         for h in range(HALVES):
             js = slice(h * JH, (h + 1) * JH)
             woven = tile([P, JH, PACK], BF16, "x1_woven%d" % h)
@@ -170,54 +163,67 @@ def tile_list_outcomegatedchain_codednote_kernel(
             nc.vector.quantize_mx(
                 out=codes[:].bitcast(E4M3), scales=scales[:], in_=woven[:].rearrange("p j t -> p (j t)")
             )
-            bank = ps.tile([P, PACK, JH], F32, name="a_ps%d" % h)
+            bank = ps.tile([P, PACK, JH], F32, name="a_ps%d" % h, tag="a_ps%d" % h)
             for t in range(PACK):
                 ms = slice(t * P, (t + 1) * P)
                 nc.tensor.matmul_mx(
                     out=bank[:, t, :], lhsT=w_d[:, ms].bitcast(E5M2), lhsT_scale=w_s[:, ms],
                     rhs=codes[:].bitcast(E4M3), rhs_scale=scales[:], start=True, stop=True,
                 )
-            a_ps.append(bank)
+            at = tile([P, JH, PACK], F32, "a_sb%d" % h)
+            nc.scalar.copy(out=at[:], in_=bank[:].rearrange("p t j -> p j t"))
+            a_sb.append(at)
 
-        q_ps = ps.tile([P, NT, J], F32, name="q_ps")
-        wc_bytes = wc_w[:].bitcast(U8)
-        p_sb = []
+        w2_d = tile([P, R], I32, "w2_d")
+        nc.vector.tensor_copy(out=dealt(w2_d[:]), in_=undealt(w2_w[:]))
+        b_ps = []
+        for h in range(HALVES):
+            js = slice(h * JH, (h + 1) * JH)
+            xg_w = tile([P, JH], U32, "xg_w%d" % h)
+            nc.vector.tensor_copy(out=xg_w[:], in_=xo_w[:].bitcast(U32).indirect(half(l2, h)))
+            bank = ps.tile([P, PACK, JH], F32, name="b_ps%d" % h)
+            for t in range(PACK):
+                ms = slice(t * P, (t + 1) * P)
+                nc.tensor.matmul_mx(
+                    out=bank[:, t, :], lhsT=w2_d[:, ms].bitcast(E4M3), lhsT_scale=w2_s[:, ms],
+                    rhs=xg_w[:].bitcast(E5M2), rhs_scale=xg_s[:, js], start=True, stop=True,
+                )
+            b_ps.append(bank)
+
+        hid_codes = tile([P, J], U32, "hid_codes")
+        hid_scales = tile([P, J], U8, "hid_scales")
+        p_ps = [ps.tile([P, J], F32, name="p_ps%d" % i) for i in range(NT)]
         for h in range(HALVES):
             js = slice(h * JH, (h + 1) * JH)
             hid = tile([P, JH, PACK], BF16, "hid%d" % h)
             nc.vector.tensor_tensor(
-                out=hid[:], in0=a_ps[h][:].rearrange("p t j -> p j t"), in1=b_sb[h][:], op=ALU.max
+                out=hid[:], in0=b_ps[h][:].rearrange("p t j -> p j t"), in1=a_sb[h][:], op=ALU.max
             )
-            codes = tile([P, JH], U32, "hid_codes%d" % h)
-            scales = tile([P, JH], U8, "hid_scales%d" % h)
             nc.vector.quantize_mx(
-                out=codes[:].bitcast(E5M2), scales=scales[:], in_=hid[:].rearrange("p j t -> p (j t)")
+                out=hid_codes[:, js].bitcast(E5M2), scales=hid_scales[:, js],
+                in_=hid[:].rearrange("p j t -> p (j t)"),
             )
-            p_ps = [
-                ps.tile([P, JH], F32, name="p_ps%d%d" % (h, i), tag=("b_ps%d" % i if h == 0 else "p_ps%d" % i))
-                for i in range(NT)
-            ]
             for i in range(NT):
                 ns = slice(i * P, (i + 1) * P)
                 nc.tensor.matmul_mx(
-                    out=p_ps[i][:], lhsT=wb_w[:, ns].bitcast(E4M3), lhsT_scale=wb_plane[:, ns],
-                    rhs=codes[:].bitcast(E5M2), rhs_scale=scales[:], start=True, stop=True,
+                    out=p_ps[i][:, js], lhsT=wb_w[:, ns].bitcast(E4M3), lhsT_scale=wb_plane[:, ns],
+                    rhs=hid_codes[:, js].bitcast(E5M2), rhs_scale=hid_scales[:, js], start=True, stop=True,
                 )
-            for i in range(NT):
-                ns = slice(i * P, (i + 1) * P)
-                nc.tensor.matmul_mx(
-                    out=q_ps[:, i, js], lhsT=wc_bytes[:, 2 * i * P : 2 * (i + 1) * P].bitcast(E2M1),
-                    lhsT_scale=wc_plane[:, ns],
-                    rhs=codes[:].bitcast(E5M2), rhs_scale=scales[:], start=True, stop=True,
-                )
-            pt = tile([P, JH], F32, "p_sb%d0" % h)
-            nc.scalar.copy(out=pt[:], in_=p_ps[0][:])
-            nc.scalar.activation(out=boards[0][:].indirect(half(l3, h)), in_=pt[:], func=ACT.Copy)
-            p_sb.append(p_ps[1])
-        for h in range(HALVES):
-            pt = tile([P, JH], F32, "p_sb%d1" % h)
-            nc.vector.tensor_copy(out=pt[:], in_=p_sb[h][:])
-            nc.vector.tensor_copy(out=boards[1][:].indirect(half(l3, h)), in_=pt[:])
+        q_ps = ps.tile([P, NT, J], F32, name="q_ps")
+        wc_bytes = wc_w[:].bitcast(U8)
+        for i in range(NT):
+            ns = slice(i * P, (i + 1) * P)
+            nc.tensor.matmul_mx(
+                out=q_ps[:, i, :], lhsT=wc_bytes[:, 2 * i * P : 2 * (i + 1) * P].bitcast(E2M1),
+                lhsT_scale=wc_plane[:, ns],
+                rhs=hid_codes[:].bitcast(E5M2), rhs_scale=hid_scales[:], start=True, stop=True,
+            )
+
+        p_sb = [tile([P, J], F32, "p_sb%d" % i) for i in range(NT)]
+        nc.scalar.copy(out=p_sb[0][:], in_=p_ps[0][:])
+        nc.vector.tensor_copy(out=p_sb[1][:], in_=p_ps[1][:])
+        nc.scalar.activation(out=boards[0][:].indirect(l3[:]), in_=p_sb[0][:], func=ACT.Copy)
+        nc.vector.tensor_copy(out=boards[1][:].indirect(l3[:]), in_=p_sb[1][:])
 
         picked = [tile([P, J], F32, "picked%d" % i) for i in range(NT)]
         nc.scalar.activation(out=picked[0][:], in_=boards[0][:].indirect(l4[:]), func=ACT.Copy)

from contextlib import ExitStack

import concourse.mybir as mybir

K, T, J, R, F, Z, N, C, O = 512, 1024, 256, 512, 512, 1024, 256, 512, 128
FLOPS = 2 * J * (K * R + F * R + 2 * R * N)

F32 = mybir.dt.float32
BF16 = mybir.dt.bfloat16
I32 = mybir.dt.int32
U32 = mybir.dt.uint32
U16 = mybir.dt.uint16
U8 = mybir.dt.uint8
E4M3 = mybir.dt.float8_e4m3fn_x4
E5M2 = mybir.dt.float8_e5m2_x4
E2M1 = mybir.dt.float4_e2m1fn_x4
ACT = mybir.ActivationFunctionType
ALU = mybir.AluOpType

P = 128
PACK = 4
QUADS = 4
HALVES = 2
JH = J // HALVES
NT = N // P
LIST_ROWS = 16


def tile_list_outcomegatedchain_codednote_kernel(
    tc, xo_words, xo_scales, cq, gs, w_words, w_scales, w2_words, w2_scales, wb_words, wb_scales,
    wc_words, wc_scales, so, sp, bo, offs, offs2, offs3, offs4, offs5, offs6, out,
):
    nc = tc.nc
    with ExitStack() as ctx:
        sb = ctx.enter_context(tc.tile_pool(name="sb", bufs=1))
        ps = ctx.enter_context(tc.psum_pool(name="ps", bufs=1))

        def tile(shape, dtype, name, tag=None):
            return sb.tile(shape, dtype, name=name, tag=tag or name, align_bytes=64)

        def load_list(src, name):
            t = sb.tile(list(src.shape), U16, name=name)
            nc.sync.dma_start(out=t[:], in_=src)
            return t

        def load_words(src, name):
            flat = src[0] if src.ndim == 3 else src[0].rearrange("p c t -> p (c t)")
            t = tile([P, flat.shape[1] // 4], I32, name)
            nc.sync.dma_start(out=t[:], in_=flat.bitcast(I32))
            return t

        def load_scale_rows(queue, src, name):
            width = src.shape[2] // 4
            t = tile([PACK, QUADS, width], I32, name)
            queue.dma_start(out=t[:], in_=src[0].bitcast(I32).rearrange("(q r) w -> r q w", r=PACK))
            return t

        def load_scale_pair(queue, first, second, name):
            width = first.shape[2] // 4
            t = tile([PACK, QUADS, 2 * width], I32, name)
            for u, src in enumerate((first, second)):
                queue.dma_start(
                    out=t[:, :, u * width : (u + 1) * width],
                    in_=src[0].bitcast(I32).rearrange("(q r) w -> r q w", r=PACK),
                )
            return t

        def zeroed_plane(width, name, tag=None):
            t = tile([P, width], U8, name, tag)
            nc.vector.memset(t[:].bitcast(I32), 0)
            return t

        def spread(plane, rows):
            for q in range(QUADS):
                nc.vector.tensor_copy(out=plane[32 * q : 32 * q + PACK, :].bitcast(I32), in_=rows[:, q, :])

        def dealt(dst):
            return dst.rearrange("p (t m) -> p m t", t=PACK)

        def undealt(src):
            return src.rearrange("p (m t) -> p m t", t=PACK)

        def half(lst, h):
            cols = JH // LIST_ROWS
            return lst[:, h * cols : (h + 1) * cols]

        cq_rows = cq.rearrange("(p t) c -> p t c", t=PACK)

        def load_cq(t):
            ct = tile([P, T], F32, "cq%d" % t)
            nc.sync.dma_start(out=ct[:], in_=cq_rows[:, t, :])
            return ct

        gs_t = tile([P, PACK], F32, "gs_t")
        nc.scalar.dma_start(out=gs_t[:], in_=gs.rearrange("(p t) o -> p (t o)", t=PACK))
        xo_rows = load_scale_rows(nc.scalar, xo_scales, "xo_rows")
        in_rows = load_scale_pair(nc.scalar, w_scales, w2_scales, "in_rows")
        out_rows = load_scale_pair(nc.scalar, wb_scales, wc_scales, "out_rows")

        l1 = load_list(offs, "l1")
        cq_t = [load_cq(0), load_cq(1)]
        l2 = load_list(offs2, "l2")
        cq_t.extend([load_cq(2), load_cq(3)])
        w_w = load_words(w_words, "w_w")
        w2_w = load_words(w2_words, "w2_w")
        xo_w = load_words(xo_words, "xo_w")
        wb_w = load_words(wb_words, "wb_w")
        wc_w = load_words(wc_words, "wc_w")
        l3 = load_list(offs3, "l3")
        l4 = load_list(offs4, "l4")
        l6 = load_list(offs6, "l6")
        l5 = load_list(offs5, "l5")
        per_n = []
        with nc.allow_non_contiguous_dma(reason="one float32 value for each output feature"):
            for src, name in ((sp, "sp_t"), (bo, "bo_t"), (so, "so_t")):
                vt = tile([P, NT], F32, name)
                nc.sync.dma_start(out=vt[:], in_=src.rearrange("(i p) o -> p (i o)", p=P))
                per_n.append(vt)
        sp_t, bo_t, so_t = per_n

        xo_plane = zeroed_plane(Z, "xo_plane")
        in_plane = zeroed_plane(2 * R, "in_plane")
        out_plane = zeroed_plane(2 * N, "out_plane")
        idle = tile([P, 2], F32, "idle")
        nc.vector.memset(idle[:, 0:1], 0.0)
        nc.scalar.activation(out=idle[:, 1:2], in_=idle[:, 0:1], func=ACT.Sigmoid)
        boards = []
        for i in range(NT):
            bd = tile([P, C], F32, "board%d" % i)
            nc.vector.memset(bd[:], 0.0)
            boards.append(bd)

        spread(xo_plane, xo_rows)
        xg_s = tile([P, J], U8, "xg_s")
        nc.vector.tensor_copy(out=xg_s[:], in_=xo_plane[:].indirect(l2[:]))
        spread(in_plane, in_rows)
        in_s = tile([P, 2 * R], U8, "in_s")
        nc.vector.tensor_copy(
            out=in_s[:].rearrange("p (u t m) -> p u m t", u=2, t=PACK),
            in_=in_plane[:].rearrange("p (u m t) -> p u m t", u=2, t=PACK),
        )
        w_s = in_s[:, :R]
        w2_s = in_s[:, R:]
        spread(out_plane, out_rows)
        wb_plane = out_plane[:, :N]
        wc_plane = out_plane[:, N:]

        x1 = tile([P, PACK, J], BF16, "x1")
        for t in range(PACK):
            nc.scalar.activation(
                out=x1[:, t, :], in_=cq_t[t][:].indirect(l1[:]), func=ACT.Copy, scale=gs_t[:, t : t + 1]
            )
        w_d = tile([P, R], U32, "w_d")
        nc.scalar.copy(out=dealt(w_d[:]), in_=undealt(w_w[:].bitcast(U32)))

        a_sb = []
        for h in range(HALVES):
            js = slice(h * JH, (h + 1) * JH)
            woven = tile([P, JH, PACK], BF16, "x1_woven%d" % h)
            nc.vector.tensor_copy(out=woven[:], in_=x1[:, :, js].rearrange("p t j -> p j t"))
            codes = tile([P, JH], U32, "x1_codes%d" % h)
            scales = tile([P, JH], U8, "x1_scales%d" % h)
            nc.vector.quantize_mx(
                out=codes[:].bitcast(E4M3), scales=scales[:], in_=woven[:].rearrange("p j t -> p (j t)")
            )
            bank = ps.tile([P, PACK, JH], F32, name="a_ps%d" % h, tag="a_ps%d" % h)
            for t in range(PACK):
                ms = slice(t * P, (t + 1) * P)
                nc.tensor.matmul_mx(
                    out=bank[:, t, :], lhsT=w_d[:, ms].bitcast(E5M2), lhsT_scale=w_s[:, ms],
                    rhs=codes[:].bitcast(E4M3), rhs_scale=scales[:], start=True, stop=True,
                )
            at = tile([P, JH, PACK], F32, "a_sb%d" % h)
            nc.scalar.copy(out=at[:], in_=bank[:].rearrange("p t j -> p j t"))
            a_sb.append(at)

        w2_d = tile([P, R], I32, "w2_d")
        nc.vector.tensor_copy(out=dealt(w2_d[:]), in_=undealt(w2_w[:]))
        b_ps = []
        for h in range(HALVES):
            js = slice(h * JH, (h + 1) * JH)
            xg_w = tile([P, JH], U32, "xg_w%d" % h)
            nc.vector.tensor_copy(out=xg_w[:], in_=xo_w[:].bitcast(U32).indirect(half(l2, h)))
            bank = ps.tile([P, PACK, JH], F32, name="b_ps%d" % h)
            for t in range(PACK):
                ms = slice(t * P, (t + 1) * P)
                nc.tensor.matmul_mx(
                    out=bank[:, t, :], lhsT=w2_d[:, ms].bitcast(E4M3), lhsT_scale=w2_s[:, ms],
                    rhs=xg_w[:].bitcast(E5M2), rhs_scale=xg_s[:, js], start=True, stop=True,
                )
            b_ps.append(bank)

        hid_codes = tile([P, J], U32, "hid_codes")
        hid_scales = tile([P, J], U8, "hid_scales")
        p_ps = [ps.tile([P, J], F32, name="p_ps%d" % i) for i in range(NT)]
        for h in range(HALVES):
            js = slice(h * JH, (h + 1) * JH)
            hid = tile([P, JH, PACK], BF16, "hid%d" % h)
            nc.vector.tensor_tensor(
                out=hid[:], in0=b_ps[h][:].rearrange("p t j -> p j t"), in1=a_sb[h][:], op=ALU.max
            )
            nc.vector.quantize_mx(
                out=hid_codes[:, js].bitcast(E5M2), scales=hid_scales[:, js],
                in_=hid[:].rearrange("p j t -> p (j t)"),
            )
            for i in range(NT):
                ns = slice(i * P, (i + 1) * P)
                nc.tensor.matmul_mx(
                    out=p_ps[i][:, js], lhsT=wb_w[:, ns].bitcast(E4M3), lhsT_scale=wb_plane[:, ns],
                    rhs=hid_codes[:, js].bitcast(E5M2), rhs_scale=hid_scales[:, js], start=True, stop=True,
                )
        q_ps = ps.tile([P, NT, J], F32, name="q_ps")
        wc_bytes = wc_w[:].bitcast(U8)
        for i in range(NT):
            ns = slice(i * P, (i + 1) * P)
            nc.tensor.matmul_mx(
                out=q_ps[:, i, :], lhsT=wc_bytes[:, 2 * i * P : 2 * (i + 1) * P].bitcast(E2M1),
                lhsT_scale=wc_plane[:, ns],
                rhs=hid_codes[:].bitcast(E5M2), rhs_scale=hid_scales[:], start=True, stop=True,
            )

        p_sb = [tile([P, J], F32, "p_sb%d" % i) for i in range(NT)]
        nc.scalar.copy(out=p_sb[0][:], in_=p_ps[0][:])
        nc.vector.tensor_copy(out=p_sb[1][:], in_=p_ps[1][:])
        nc.scalar.activation(out=boards[0][:].indirect(l3[:]), in_=p_sb[0][:], func=ACT.Copy)
        nc.vector.tensor_copy(out=boards[1][:].indirect(l3[:]), in_=p_sb[1][:])

        picked = [tile([P, J], F32, "picked%d" % i) for i in range(NT)]
        nc.scalar.activation(out=picked[0][:], in_=boards[0][:].indirect(l4[:]), func=ACT.Copy)
        nc.vector.tensor_copy(out=picked[1][:], in_=boards[1][:].indirect(l4[:]))

        for i in range(NT):
            m0 = tile([P, J], F32, "m0_%d" % i)
            nc.vector.tensor_tensor(out=m0[:], in0=q_ps[:, i, :], in1=picked[i][:], op=ALU.max)
            gate = tile([P, O], F32, "gate%d" % i)
            nc.scalar.activation(
                out=gate[:], in_=m0[:].indirect(l6[:]), func=ACT.Sigmoid,
                scale=sp_t[:, i : i + 1], bias=bo_t[:, i : i + 1],
            )
            kept = tile([P, O], F32, "kept%d" % i)
            nc.scalar.activation(
                out=kept[:], in_=m0[:].indirect(l5[:]), func=ACT.Copy, scale=so_t[:, i : i + 1]
            )
            y = tile([P, O], F32, "y%d" % i)
            nc.vector.tensor_tensor(out=y[:], in0=kept[:], in1=gate[:], op=ALU.mult)
            nc.sync.dma_start(out=out[i * P : (i + 1) * P, :], in_=y[:])
